import numpy as np
import ml_dtypes


def mxq(x, axis, fmt="e4m3"):
    dtype, down = {"e4m3": (ml_dtypes.float8_e4m3fn, 7), "e5m2": (ml_dtypes.float8_e5m2, 14)}[fmt]
    v = np.moveaxis(np.asarray(x, np.float32).astype(ml_dtypes.bfloat16).astype(np.float64), axis, -1)
    blocks = v.reshape(v.shape[:-1] + (-1, 32))
    amax = np.abs(blocks).max(-1, keepdims=True)
    byte = np.maximum(np.where(amax > 0, np.frexp(amax)[1] - 1 + 127, 0) - down, 1)
    scale = np.exp2(byte - 127.0)
    codes = (blocks / scale).astype(np.float32).astype(dtype).astype(np.float64)
    return np.moveaxis((codes * scale).reshape(v.shape), -1, axis)


WIDE = False


def mx_kscale(k):
    if not WIDE:
        return np.ones(k)
    levels = np.array([10, -10, 5, -5, 0])
    if k % 512:
        return np.exp2(np.random.permutation(np.resize(levels, k // 32))).repeat(32)
    a = np.empty((k // 512, 16))
    for p in range(k // 512):
        a[p, :8] = np.random.permutation(np.resize(levels, 8))
        for g in range(8):
            far = levels[np.abs(levels - a[p, g]) >= 10]
            a[p, g + 8] = far[np.random.randint(len(far))]
    return np.exp2(a.ravel()).repeat(32)


def f64(x):
    return np.asarray(x).astype(np.float64)


def striped(idx):
    return np.tile(np.asarray(idx).reshape(-1, 16).T, (8, 1)).astype(np.uint16)


def unstriped(offs):
    return offs[:16].T.reshape(-1).astype(np.int64)


E2M1 = np.array([0.0, 0.5, 1.0, 1.5, 2.0, 3.0, 4.0, 6.0, -0.0, -0.5, -1.0, -1.5, -2.0, -3.0, -4.0, -6.0])


def pack_weight(w, fmt):
    k, n = w.shape
    w = f64(np.asarray(w, np.float32).astype(ml_dtypes.bfloat16)).reshape(k // 32, 32, n)
    amax = np.abs(w).max(1)
    if fmt == "e4m3":
        byte = np.frexp(amax)[1] - 1 + 127 - 7
    else:
        mant, ex = np.frexp(amax / 6.0)
        byte = np.where(mant > 0.5, ex, ex - 1) + 127
    byte = np.clip(np.where(amax > 0, byte, 1), 1, 254)
    scaled = (w * np.exp2(127.0 - byte)[:, None, :]).reshape(k, n).astype(np.float32)
    by_word = np.ascontiguousarray(scaled.reshape(k // 512, 128, 4, n).transpose(0, 1, 3, 2))
    if fmt == "e4m3":
        words = by_word.astype(ml_dtypes.float8_e4m3fn).view(np.uint8)
    else:
        c = by_word.astype(ml_dtypes.float4_e2m1fn).view(np.uint8) & 0xF
        words = (c[..., 0::2] | (c[..., 1::2] << 4)).reshape(k // 512, 128, 2 * n)
    return np.ascontiguousarray(words), np.ascontiguousarray(byte.astype(np.uint8).reshape(k // 512, 16, n))


def unpack_weight(words, scales, fmt):
    g, _, n = scales.shape
    words = np.ascontiguousarray(words).reshape(g, 128, n, -1)
    if fmt == "e4m3":
        vals = words.view(ml_dtypes.float8_e4m3fn).astype(np.float64)
    else:
        nib = np.empty((g, 128, n, 4), np.uint8)
        nib[..., 0::2] = words & 0xF
        nib[..., 1::2] = words >> 4
        vals = E2M1[nib]
    vals = vals * np.repeat(np.exp2(scales.astype(np.float64) - 127.0), 8, axis=1)[..., None]
    return vals.transpose(0, 1, 3, 2).reshape(g * 512, n)


D, E, T, I, Q = 512, 512, 2048, 512, 128


def setup_inputs():
    n = np.random.standard_normal
    idx = np.random.permutation(T)[:I]
    fd = mx_kscale(D)
    fi = mx_kscale(I)
    ti = np.ones(T)
    ti[idx] = fi
    keysp = pack_weight(n((D, T)) / fd[:, None], "e4m3")
    return {
        "query": (n((D, Q)) * 0.5 / np.sqrt(D) * fd[:, None]).astype(np.float32),
        "dquery": (n((D, Q)) * 1.0 / np.sqrt(D) * fd[:, None]).astype(np.float32),
        "keys_words": keysp[0],
        "keys_scales": keysp[1],
        "size": (np.random.uniform(4.0, 16.0, (1, I)) * fi).astype(np.float32),
        "vals": (n((E, T)) / ti).astype(np.float32),
        "offs": striped(idx),
    }


def reference(query, dquery, keys_words, keys_scales, size, vals, offs):
    idx = unstriped(offs)
    keysu = unpack_weight(keys_words, keys_scales, "e4m3")
    queryq = mxq(f64(query), 0, "e4m3")
    keysidxg = keysu[:, idx]
    a = queryq.T @ keysidxg
    dqueryq = mxq(f64(dquery), 0, "e4m3")
    b = dqueryq.T @ keysidxg
    p = np.exp(a - np.max(a, axis=1, keepdims=True))
    w = p / np.sum(p, axis=1, keepdims=True)
    dw = w * (b - np.sum(w * b, axis=1, keepdims=True)) * f64(size)
    wt = dw.T
    vt = f64(vals)[:, idx].T
    wtq = mxq(wt, 0, "e4m3")
    vtq = mxq(vt, 0, "e4m3")
    o = wtq.T @ vtq
    return o

@@ -1,0 +1,166 @@
+from contextlib import ExitStack
+
+import concourse.mybir as mybir
+from concourse.masks import make_identity
+
+D, E, T, I, Q = 512, 512, 2048, 512, 128
+FLOPS = 3 * 2 * 512 * 512 * 128
+
+F32 = mybir.dt.float32
+BF16 = mybir.dt.bfloat16
+I32 = mybir.dt.int32
+U32 = mybir.dt.uint32
+U16 = mybir.dt.uint16
+U8 = mybir.dt.uint8
+FP8X4 = mybir.dt.float8_e4m3fn_x4
+ALU = mybir.AluOpType
+ACT = mybir.ActivationFunctionType
+AX = mybir.AxisListType
+
+P = 128
+PACK = 4
+BLOCKS = E // P
+
+
+def tile_attend_readtangent_kernel(tc, query, dquery, keys_words, keys_scales, size, vals, offs, out):
+    nc = tc.nc
+    with ExitStack() as ctx:
+        sb = ctx.enter_context(tc.tile_pool(name="sb", bufs=1))
+        ps = ctx.enter_context(tc.psum_pool(name="ps", bufs=1))
+        ps_turn = ctx.enter_context(tc.psum_pool(name="ps_turn", bufs=2))
+
+        offsets = sb.tile([P, I // 16], U16, name="offsets")
+        nc.sync.dma_start(offsets[:], offs)
+
+        key_scale_pool = sb.tile([P, T], U8, name="key_scale_pool", tag="key_bytes", align_bytes=64)
+        nc.vector.memset(key_scale_pool[:].bitcast(I32), 0)
+        for quad in range(4):
+            nc.scalar.dma_start(
+                key_scale_pool[32 * quad : 32 * quad + 4, :].bitcast(I32),
+                keys_scales[0, 4 * quad : 4 * quad + 4, :].bitcast(I32),
+            )
+
+        size_cols = sb.tile([P, PACK], F32, name="size_cols")
+        nc.sync.dma_start(size_cols[:], size[0].rearrange("(p t) -> p t", t=PACK))
+
+        key_word_pool = sb.tile([P, T], I32, name="key_word_pool", tag="key_word_pool", align_bytes=64)
+        nc.sync.dma_start(key_word_pool[:], keys_words[0].rearrange("p n t -> p (n t)").bitcast(I32))
+
+        raw_q = []
+        for name, src, tag in (("q", query, "val1"), ("dq", dquery, "val2")):
+            raw = sb.tile([P, PACK, Q], F32, name="raw_" + name, tag=tag, align_bytes=64)
+            nc.sync.dma_start(raw[:], src.rearrange("(p j) q -> p j q", j=PACK))
+            raw_q.append(raw)
+
+        ident = sb.tile([P, P], F32, name="ident")
+        make_identity(nc, ident[:])
+
+        warm_in = sb.tile([P, 1], F32, name="warm_in", tag="val0", align_bytes=64)
+        warm_out = sb.tile([P, 1], F32, name="warm_out")
+        nc.vector.memset(warm_in[:], 0.0)
+        nc.scalar.activation(warm_out[:], warm_in[:], ACT.Exp)
+
+        def quantise(name, grouped, width, tag):
+            codes = sb.tile([P, width], U32, name=name + "_codes", tag=tag, align_bytes=64)
+            scales = sb.tile([P, width], U8, name=name + "_scales", align_bytes=64)
+            nc.vector.quantize_mx(out=codes[:].bitcast(FP8X4), scales=scales[:], in_=grouped)
+            return codes, scales
+
+        grouped_q = []
+        for name, raw, tag in zip(("q", "dq"), raw_q, ("grouped_q", "val3")):
+            grouped = sb.tile([P, Q, PACK], BF16, name="grouped_" + name, tag=tag, align_bytes=64)
+            nc.scalar.copy(grouped[:], raw[:].rearrange("p j q -> p q j"))
+            grouped_q.append(quantise(name, grouped[:].rearrange("p q j -> p (q j)"), Q, name + "_codes"))
+
+        size_rows = ps.tile([P, PACK, P], F32, name="size_rows")
+        for t in range(PACK):
+            nc.tensor.transpose(size_rows[:, t, :], size_cols[:, t : t + 1].to_broadcast([P, P]), ident[:])
+
+        val_pool = []
+        for blk in range(BLOCKS):
+            pool_blk = sb.tile([P, T], F32, name="val_pool%d" % blk, tag="val%d" % blk, align_bytes=64)
+            nc.sync.dma_start(pool_blk[:], vals[blk * P : (blk + 1) * P, :])
+            val_pool.append(pool_blk)
+
+        key_scales = sb.tile([P, I], U8, name="key_scales", align_bytes=64)
+        nc.vector.tensor_copy(key_scales[:], key_scale_pool[:].indirect(offsets[:]))
+        key_words = sb.tile([P, I], U32, name="key_words", tag="key_bytes", align_bytes=64)
+        nc.vector.tensor_copy(key_words[:], key_word_pool[:].bitcast(U32).indirect(offsets[:]))
+
+        scores = []
+        for name, (codes, scales) in zip(("q", "dq"), grouped_q):
+            bank = ps.tile([P, I], F32, name="score_" + name)
+            nc.tensor.matmul_mx(
+                out=bank[:], lhsT=codes[:].bitcast(FP8X4), lhsT_scale=scales[:],
+                rhs=key_words[:].bitcast(FP8X4), rhs_scale=key_scales[:], start=True, stop=True,
+            )
+            scores.append(bank)
+        a_bank, b_bank = scores
+
+        def turn(rows, grouped):
+            words = rows[:].bitcast(F32)
+            turned = ps_turn.tile([P, 2, P], F32, name="turned")
+            for u in range(2):
+                nc.tensor.transpose(turned[:, u, :], words[:, u : I // 2 : 2], ident[:])
+            nc.scalar.copy(
+                grouped.bitcast(F32).rearrange("p (c u) -> p c u", u=2),
+                turned[:].rearrange("p u c -> p c u"),
+            )
+
+        def gather_vals(blk, grouped):
+            picked = sb.tile([P, I], BF16, name="picked%d" % blk, align_bytes=64)
+            nc.vector.tensor_copy(picked[:], val_pool[blk][:].indirect(offsets[:]))
+            turn(picked, grouped)
+
+        width = P * PACK
+        grouped_wv = sb.tile([P, 2 * width], BF16, name="grouped_wv", align_bytes=64)
+        grouped_v = [grouped_wv[:, width:]] + [
+            sb.tile([P, width], BF16, name="grouped_v%d" % blk, align_bytes=64)[:] for blk in range(1, BLOCKS)
+        ]
+        gather_vals(0, grouped_v[0])
+
+        neg_max = sb.tile([P, 1], F32, name="neg_max")
+        nc.vector.tensor_reduce(neg_max[:], a_bank[:], AX.X, ALU.max, negate=True)
+        p = sb.tile([P, I], F32, name="p")
+        row_sum = sb.tile([P, 1], F32, name="row_sum")
+        nc.scalar.activation(p[:], a_bank[:], ACT.Exp, bias=neg_max[:], accum_out=row_sum[:])
+        inv_sum = sb.tile([P, 1], F32, name="inv_sum", tag="val0", align_bytes=64)
+        nc.vector.reciprocal(inv_sum[:], row_sum[:])
+        wb = sb.tile([P, I], F32, name="wb")
+        mean_b = sb.tile([P, 1], F32, name="mean_b")
+        nc.vector.scalar_tensor_tensor(wb[:], p[:], inv_sum[:], b_bank[:], ALU.mult, ALU.mult, accum_out=mean_b[:])
+        w_size = sb.tile([P, I], F32, name="w_size")
+        nc.vector.scalar_tensor_tensor(
+            w_size[:].rearrange("q (s t) -> q s t", t=PACK),
+            p[:].rearrange("q (s t) -> q s t", t=PACK),
+            inv_sum[:],
+            size_rows[:].rearrange("q t s -> q s t"),
+            ALU.mult, ALU.mult,
+        )
+        dw = sb.tile([P, I], BF16, name="dw", align_bytes=64)
+        nc.vector.scalar_tensor_tensor(dw[:], b_bank[:], mean_b[:], w_size[:], ALU.subtract, ALU.mult)
+        turn(dw, grouped_wv[:, :width])
+
+        gather_vals(1, grouped_v[1])
+        wv_codes, wv_scales = quantise("wv", grouped_wv[:], 2 * P, "val1")
+        w_codes, w_scales = wv_codes[:, :P], wv_scales[:, :P]
+        v_quant = [(wv_codes[:, P:], wv_scales[:, P:])]
+        for blk in range(1, BLOCKS):
+            last = blk == BLOCKS - 1
+            if not last:
+                gather_vals(blk + 1, grouped_v[blk + 1])
+            codes, scales = quantise("v%d" % blk, grouped_v[blk], P, "v_last" if last else "val%d" % (blk + 1))
+            v_quant.append((codes[:], scales[:]))
+
+        result = sb.tile([P, E], F32, name="result")
+        for blocks, copy_out in (((0, 1), nc.scalar.copy), ((2,), nc.vector.tensor_copy), ((3,), nc.scalar.copy)):
+            bank = ps.tile([P, len(blocks) * P], F32, name="out%d" % blocks[0])
+            for j, blk in enumerate(blocks):
+                v_codes, v_scales = v_quant[blk]
+                nc.tensor.matmul_mx(
+                    out=bank[:, j * P : (j + 1) * P], lhsT=w_codes.bitcast(FP8X4), lhsT_scale=w_scales,
+                    rhs=v_codes.bitcast(FP8X4), rhs_scale=v_scales, start=True, stop=True,
+                )
+            cols = slice(blocks[0] * P, (blocks[-1] + 1) * P)
+            copy_out(result[:, cols], bank[:])
+            nc.sync.dma_start(out[:, cols], result[:, cols])

@@ -3,7 +3,7 @@ from contextlib import ExitStack
 import concourse.mybir as mybir
 from concourse.masks import make_identity
 
-D, E, T, I, Q = 512, 512, 2048, 512, 128
+E, T, I, Q = 512, 2048, 512, 128
 FLOPS = 3 * 2 * 512 * 512 * 128
 
 F32 = mybir.dt.float32
@@ -20,6 +20,7 @@ AX = mybir.AxisListType
 P = 128
 PACK = 4
 BLOCKS = E // P
+WIDTH = P * PACK
 
 
 def tile_attend_readtangent_kernel(tc, query, dquery, keys_words, keys_scales, size, vals, offs, out):
@@ -29,10 +30,13 @@ def tile_attend_readtangent_kernel(tc, query, dquery, keys_words, keys_scales, s
         ps = ctx.enter_context(tc.psum_pool(name="ps", bufs=1))
         ps_turn = ctx.enter_context(tc.psum_pool(name="ps_turn", bufs=2))
 
-        offsets = sb.tile([P, I // 16], U16, name="offsets")
+        def tile(shape, dtype, name, tag=None):
+            return sb.tile(shape, dtype, name=name, tag=tag or name, align_bytes=64)
+
+        offsets = tile([P, I // 16], U16, "offsets")
         nc.sync.dma_start(offsets[:], offs)
 
-        key_scale_pool = sb.tile([P, T], U8, name="key_scale_pool", tag="key_bytes", align_bytes=64)
+        key_scale_pool = tile([P, T], U8, "key_scale_pool")
         nc.vector.memset(key_scale_pool[:].bitcast(I32), 0)
         for quad in range(4):
             nc.scalar.dma_start(
@@ -40,62 +44,68 @@ def tile_attend_readtangent_kernel(tc, query, dquery, keys_words, keys_scales, s
                 keys_scales[0, 4 * quad : 4 * quad + 4, :].bitcast(I32),
             )
 
-        size_cols = sb.tile([P, PACK], F32, name="size_cols")
-        nc.sync.dma_start(size_cols[:], size[0].rearrange("(p t) -> p t", t=PACK))
-
-        key_word_pool = sb.tile([P, T], I32, name="key_word_pool", tag="key_word_pool", align_bytes=64)
+        key_word_pool = tile([P, T], I32, "key_word_pool")
         nc.sync.dma_start(key_word_pool[:], keys_words[0].rearrange("p n t -> p (n t)").bitcast(I32))
 
         raw_q = []
-        for name, src, tag in (("q", query, "val1"), ("dq", dquery, "val2")):
-            raw = sb.tile([P, PACK, Q], F32, name="raw_" + name, tag=tag, align_bytes=64)
+        for name, src, tag in (("raw_q", query, "val2"), ("raw_dq", dquery, "val3")):
+            raw = tile([P, PACK, Q], F32, name, tag)
             nc.sync.dma_start(raw[:], src.rearrange("(p j) q -> p j q", j=PACK))
             raw_q.append(raw)
 
-        ident = sb.tile([P, P], F32, name="ident")
+        size_cols = tile([P, PACK], F32, "size_cols")
+        nc.sync.dma_start(size_cols[:], size[0].rearrange("(p t) -> p t", t=PACK))
+
+        ident = tile([P, P], F32, "ident")
         make_identity(nc, ident[:])
 
-        warm_in = sb.tile([P, 1], F32, name="warm_in", tag="val0", align_bytes=64)
-        warm_out = sb.tile([P, 1], F32, name="warm_out")
+        warm_in = tile([P, 1], F32, "warm_in", "val0")
+        warm_out = tile([P, 1], F32, "warm_out", "val1")
         nc.vector.memset(warm_in[:], 0.0)
         nc.scalar.activation(warm_out[:], warm_in[:], ACT.Exp)
 
-        def quantise(name, grouped, width, tag):
-            codes = sb.tile([P, width], U32, name=name + "_codes", tag=tag, align_bytes=64)
-            scales = sb.tile([P, width], U8, name=name + "_scales", align_bytes=64)
-            nc.vector.quantize_mx(out=codes[:].bitcast(FP8X4), scales=scales[:], in_=grouped)
+        def quantise(name, grouped, tag=None):
+            words = grouped.shape[1] // PACK
+            codes = tile([P, words], U32, name + "_codes", tag)
+            scales = tile([P, words], U8, name + "_scales")
+            nc.vector.quantize_mx(out=codes[:].bitcast(FP8X4), scales=scales[:], in_=grouped[:])
             return codes, scales
 
-        grouped_q = []
-        for name, raw, tag in zip(("q", "dq"), raw_q, ("grouped_q", "val3")):
-            grouped = sb.tile([P, Q, PACK], BF16, name="grouped_" + name, tag=tag, align_bytes=64)
-            nc.scalar.copy(grouped[:], raw[:].rearrange("p j q -> p q j"))
-            grouped_q.append(quantise(name, grouped[:].rearrange("p q j -> p (q j)"), Q, name + "_codes"))
+        grouped_q = tile([P, 2 * WIDTH], BF16, "grouped_q")
+        for j, raw in enumerate(raw_q):
+            nc.scalar.copy(
+                grouped_q[:, j * WIDTH : (j + 1) * WIDTH].rearrange("p (q j) -> p q j", j=PACK),
+                raw[:].rearrange("p j q -> p q j"),
+            )
+
+        key_words = tile([P, I], U32, "key_words")
+        nc.vector.tensor_copy(key_words[:], key_word_pool[:].bitcast(U32).indirect(offsets[:]))
+        key_scales = tile([P, I], U8, "key_scales")
+        nc.vector.tensor_copy(key_scales[:], key_scale_pool[:].indirect(offsets[:]))
+        q_codes, q_scales = quantise("q", grouped_q)
+
+        val_pool = []
+        for blk in range(BLOCKS):
+            pool_blk = tile([P, T], F32, "val_pool%d" % blk, "val%d" % blk)
+            nc.sync.dma_start(pool_blk[:], vals[blk * P : (blk + 1) * P, :])
+            val_pool.append(pool_blk)
+
+        def product(bank, lhs, lhs_cols, rhs, rhs_cols):
+            nc.tensor.matmul_mx(
+                out=bank,
+                lhsT=lhs[0][:, lhs_cols].bitcast(FP8X4), lhsT_scale=lhs[1][:, lhs_cols],
+                rhs=rhs[0][:, rhs_cols].bitcast(FP8X4), rhs_scale=rhs[1][:, rhs_cols],
+                start=True, stop=True,
+            )
+
+        a_bank = ps.tile([P, I], F32, name="a_bank")
+        b_bank = ps.tile([P, I], F32, name="b_bank")
+        product(a_bank[:], (q_codes, q_scales), slice(0, Q), (key_words, key_scales), slice(0, I))
+        product(b_bank[:], (q_codes, q_scales), slice(Q, 2 * Q), (key_words, key_scales), slice(0, I))
 
         size_rows = ps.tile([P, PACK, P], F32, name="size_rows")
         for t in range(PACK):
             nc.tensor.transpose(size_rows[:, t, :], size_cols[:, t : t + 1].to_broadcast([P, P]), ident[:])
-
-        val_pool = []
-        for blk in range(BLOCKS):
-            pool_blk = sb.tile([P, T], F32, name="val_pool%d" % blk, tag="val%d" % blk, align_bytes=64)
-            nc.sync.dma_start(pool_blk[:], vals[blk * P : (blk + 1) * P, :])
-            val_pool.append(pool_blk)
-
-        key_scales = sb.tile([P, I], U8, name="key_scales", align_bytes=64)
-        nc.vector.tensor_copy(key_scales[:], key_scale_pool[:].indirect(offsets[:]))
-        key_words = sb.tile([P, I], U32, name="key_words", tag="key_bytes", align_bytes=64)
-        nc.vector.tensor_copy(key_words[:], key_word_pool[:].bitcast(U32).indirect(offsets[:]))
-
-        scores = []
-        for name, (codes, scales) in zip(("q", "dq"), grouped_q):
-            bank = ps.tile([P, I], F32, name="score_" + name)
-            nc.tensor.matmul_mx(
-                out=bank[:], lhsT=codes[:].bitcast(FP8X4), lhsT_scale=scales[:],
-                rhs=key_words[:].bitcast(FP8X4), rhs_scale=key_scales[:], start=True, stop=True,
-            )
-            scores.append(bank)
-        a_bank, b_bank = scores
 
         def turn(rows, grouped):
             words = rows[:].bitcast(F32)
@@ -108,59 +118,54 @@ def tile_attend_readtangent_kernel(tc, query, dquery, keys_words, keys_scales, s
             )
 
         def gather_vals(blk, grouped):
-            picked = sb.tile([P, I], BF16, name="picked%d" % blk, align_bytes=64)
+            picked = tile([P, I], BF16, "picked%d" % blk)
             nc.vector.tensor_copy(picked[:], val_pool[blk][:].indirect(offsets[:]))
             turn(picked, grouped)
 
-        width = P * PACK
-        grouped_wv = sb.tile([P, 2 * width], BF16, name="grouped_wv", align_bytes=64)
-        grouped_v = [grouped_wv[:, width:]] + [
-            sb.tile([P, width], BF16, name="grouped_v%d" % blk, align_bytes=64)[:] for blk in range(1, BLOCKS)
-        ]
-        gather_vals(0, grouped_v[0])
+        val_bf16 = tile([P, T], BF16, "val_bf16")
+        nc.scalar.activation(val_bf16[:], val_pool[1][:], ACT.Copy)
+        grouped_w0 = tile([P, 2 * WIDTH], BF16, "grouped_w0", "val1")
+        grouped_12 = tile([P, 2 * WIDTH], BF16, "grouped_12")
+        grouped_3 = tile([P, WIDTH], BF16, "grouped_3")
 
-        neg_max = sb.tile([P, 1], F32, name="neg_max")
+        neg_max = tile([P, 1], F32, "neg_max")
         nc.vector.tensor_reduce(neg_max[:], a_bank[:], AX.X, ALU.max, negate=True)
-        p = sb.tile([P, I], F32, name="p")
-        row_sum = sb.tile([P, 1], F32, name="row_sum")
+        gather_vals(0, grouped_w0[:, WIDTH:])
+        p = tile([P, I], F32, "p")
+        row_sum = tile([P, 1], F32, "row_sum")
         nc.scalar.activation(p[:], a_bank[:], ACT.Exp, bias=neg_max[:], accum_out=row_sum[:])
-        inv_sum = sb.tile([P, 1], F32, name="inv_sum", tag="val0", align_bytes=64)
-        nc.vector.reciprocal(inv_sum[:], row_sum[:])
-        wb = sb.tile([P, I], F32, name="wb")
-        mean_b = sb.tile([P, 1], F32, name="mean_b")
-        nc.vector.scalar_tensor_tensor(wb[:], p[:], inv_sum[:], b_bank[:], ALU.mult, ALU.mult, accum_out=mean_b[:])
-        w_size = sb.tile([P, I], F32, name="w_size")
+        picked1 = tile([P, I], BF16, "picked1")
+        nc.scalar.activation(picked1[:], val_bf16[:].indirect(offsets[:]), ACT.Copy)
+        scratch = tile([P, I + 1], F32, "scratch", "val0")
+        pb, inv_sum = scratch[:, :I], scratch[:, I:]
+        nc.vector.reciprocal(inv_sum, row_sum[:])
+        pb_sum = tile([P, 1], F32, "pb_sum")
+        nc.vector.scalar_tensor_tensor(pb, p[:], 1.0, b_bank[:], ALU.mult, ALU.mult, accum_out=pb_sum[:])
+        w_size = tile([P, I], F32, "w_size")
         nc.vector.scalar_tensor_tensor(
             w_size[:].rearrange("q (s t) -> q s t", t=PACK),
             p[:].rearrange("q (s t) -> q s t", t=PACK),
-            inv_sum[:],
+            inv_sum,
             size_rows[:].rearrange("q t s -> q s t"),
             ALU.mult, ALU.mult,
         )
-        dw = sb.tile([P, I], BF16, name="dw", align_bytes=64)
+        mean_b = tile([P, 1], F32, "mean_b")
+        nc.vector.tensor_tensor(mean_b[:], pb_sum[:], inv_sum, ALU.mult)
+        dw = tile([P, I], BF16, "dw")
         nc.vector.scalar_tensor_tensor(dw[:], b_bank[:], mean_b[:], w_size[:], ALU.subtract, ALU.mult)
-        turn(dw, grouped_wv[:, :width])
+        turn(dw, grouped_w0[:, :WIDTH])
 
-        gather_vals(1, grouped_v[1])
-        wv_codes, wv_scales = quantise("wv", grouped_wv[:], 2 * P, "val1")
-        w_codes, w_scales = wv_codes[:, :P], wv_scales[:, :P]
-        v_quant = [(wv_codes[:, P:], wv_scales[:, P:])]
-        for blk in range(1, BLOCKS):
-            last = blk == BLOCKS - 1
-            if not last:
-                gather_vals(blk + 1, grouped_v[blk + 1])
-            codes, scales = quantise("v%d" % blk, grouped_v[blk], P, "v_last" if last else "val%d" % (blk + 1))
-            v_quant.append((codes[:], scales[:]))
+        turn(picked1, grouped_12[:, :WIDTH])
+        gather_vals(2, grouped_12[:, WIDTH:])
+        quant_w0 = quantise("w0", grouped_w0, "val2")
+        gather_vals(3, grouped_3[:])
+        quant_12 = quantise("v12", grouped_12, "val3")
+        quant_3 = quantise("v3", grouped_3)
 
-        result = sb.tile([P, E], F32, name="result")
-        for blocks, copy_out in (((0, 1), nc.scalar.copy), ((2,), nc.vector.tensor_copy), ((3,), nc.scalar.copy)):
-            bank = ps.tile([P, len(blocks) * P], F32, name="out%d" % blocks[0])
-            for j, blk in enumerate(blocks):
-                v_codes, v_scales = v_quant[blk]
-                nc.tensor.matmul_mx(
-                    out=bank[:, j * P : (j + 1) * P], lhsT=w_codes.bitcast(FP8X4), lhsT_scale=w_scales,
-                    rhs=v_codes.bitcast(FP8X4), rhs_scale=v_scales, start=True, stop=True,
-                )
-            cols = slice(blocks[0] * P, (blocks[-1] + 1) * P)
-            copy_out(result[:, cols], bank[:])
+        result = tile([P, E], F32, "result")
+        for first, count, quant, at in ((0, 1, quant_w0, P), (1, 2, quant_12, 0), (3, 1, quant_3, 0)):
+            bank = ps.tile([P, count * P], F32, name="out%d" % first)
+            product(bank[:], quant_w0, slice(0, Q), quant, slice(at, at + count * P))
+            cols = slice(first * P, (first + count) * P)
+            nc.scalar.copy(result[:, cols], bank[:])
             nc.sync.dma_start(out[:, cols], result[:, cols])

@@ -39,7 +39,7 @@ def tile_attend_readtangent_kernel(tc, query, dquery, keys_words, keys_scales, s
         key_scale_pool = tile([P, T], U8, "key_scale_pool")
         nc.vector.memset(key_scale_pool[:].bitcast(I32), 0)
         for quad in range(4):
-            nc.scalar.dma_start(
+            nc.sync.dma_start(
                 key_scale_pool[32 * quad : 32 * quad + 4, :].bitcast(I32),
                 keys_scales[0, 4 * quad : 4 * quad + 4, :].bitcast(I32),
             )
@@ -54,7 +54,7 @@ def tile_attend_readtangent_kernel(tc, query, dquery, keys_words, keys_scales, s
             raw_q.append(raw)
 
         size_cols = tile([P, PACK], F32, "size_cols")
-        nc.sync.dma_start(size_cols[:], size[0].rearrange("(p t) -> p t", t=PACK))
+        nc.gpsimd.dma_start(size_cols[:], size[0].rearrange("(p t) -> p t", t=PACK))
 
         ident = tile([P, P], F32, "ident")
         make_identity(nc, ident[:])
@@ -71,18 +71,18 @@ def tile_attend_readtangent_kernel(tc, query, dquery, keys_words, keys_scales, s
             nc.vector.quantize_mx(out=codes[:].bitcast(FP8X4), scales=scales[:], in_=grouped[:])
             return codes, scales
 
-        grouped_q = tile([P, 2 * WIDTH], BF16, "grouped_q")
-        for j, raw in enumerate(raw_q):
-            nc.scalar.copy(
-                grouped_q[:, j * WIDTH : (j + 1) * WIDTH].rearrange("p (q j) -> p q j", j=PACK),
-                raw[:].rearrange("p j q -> p q j"),
-            )
+        grouped_q = []
+        for name, raw in zip(("grouped_q", "grouped_dq"), raw_q):
+            grouped = tile([P, WIDTH], BF16, name)
+            nc.scalar.copy(grouped[:].rearrange("p (q j) -> p q j", j=PACK), raw[:].rearrange("p j q -> p q j"))
+            grouped_q.append(grouped)
 
         key_words = tile([P, I], U32, "key_words")
         nc.vector.tensor_copy(key_words[:], key_word_pool[:].bitcast(U32).indirect(offsets[:]))
         key_scales = tile([P, I], U8, "key_scales")
         nc.vector.tensor_copy(key_scales[:], key_scale_pool[:].indirect(offsets[:]))
-        q_codes, q_scales = quantise("q", grouped_q)
+        quant_q = quantise("q", grouped_q[0])
+        quant_dq = quantise("dq", grouped_q[1])
 
         val_pool = []
         for blk in range(BLOCKS):
@@ -100,8 +100,8 @@ def tile_attend_readtangent_kernel(tc, query, dquery, keys_words, keys_scales, s
 
         a_bank = ps.tile([P, I], F32, name="a_bank")
         b_bank = ps.tile([P, I], F32, name="b_bank")
-        product(a_bank[:], (q_codes, q_scales), slice(0, Q), (key_words, key_scales), slice(0, I))
-        product(b_bank[:], (q_codes, q_scales), slice(Q, 2 * Q), (key_words, key_scales), slice(0, I))
+        product(a_bank[:], quant_q, slice(0, Q), (key_words, key_scales), slice(0, I))
+        product(b_bank[:], quant_dq, slice(0, Q), (key_words, key_scales), slice(0, I))
 
         size_rows = ps.tile([P, PACK, P], F32, name="size_rows")
         for t in range(PACK):
@@ -122,9 +122,7 @@ def tile_attend_readtangent_kernel(tc, query, dquery, keys_words, keys_scales, s
             nc.vector.tensor_copy(picked[:], val_pool[blk][:].indirect(offsets[:]))
             turn(picked, grouped)
 
-        val_bf16 = tile([P, T], BF16, "val_bf16")
-        nc.scalar.activation(val_bf16[:], val_pool[1][:], ACT.Copy)
-        grouped_w0 = tile([P, 2 * WIDTH], BF16, "grouped_w0", "val1")
+        grouped_w0 = tile([P, 2 * WIDTH], BF16, "grouped_w0")
         grouped_12 = tile([P, 2 * WIDTH], BF16, "grouped_12")
         grouped_3 = tile([P, WIDTH], BF16, "grouped_3")
 
@@ -134,8 +132,6 @@ def tile_attend_readtangent_kernel(tc, query, dquery, keys_words, keys_scales, s
         p = tile([P, I], F32, "p")
         row_sum = tile([P, 1], F32, "row_sum")
         nc.scalar.activation(p[:], a_bank[:], ACT.Exp, bias=neg_max[:], accum_out=row_sum[:])
-        picked1 = tile([P, I], BF16, "picked1")
-        nc.scalar.activation(picked1[:], val_bf16[:].indirect(offsets[:]), ACT.Copy)
         scratch = tile([P, I + 1], F32, "scratch", "val0")
         pb, inv_sum = scratch[:, :I], scratch[:, I:]
         nc.vector.reciprocal(inv_sum, row_sum[:])
@@ -155,7 +151,7 @@ def tile_attend_readtangent_kernel(tc, query, dquery, keys_words, keys_scales, s
         nc.vector.scalar_tensor_tensor(dw[:], b_bank[:], mean_b[:], w_size[:], ALU.subtract, ALU.mult)
         turn(dw, grouped_w0[:, :WIDTH])
 
-        turn(picked1, grouped_12[:, :WIDTH])
+        gather_vals(1, grouped_12[:, :WIDTH])
         gather_vals(2, grouped_12[:, WIDTH:])
         quant_w0 = quantise("w0", grouped_w0, "val2")
         gather_vals(3, grouped_3[:])

@@ -64,11 +64,9 @@ def tile_attend_readtangent_kernel(tc, query, dquery, keys_words, keys_scales, s
         nc.vector.memset(warm_in[:], 0.0)
         nc.scalar.activation(warm_out[:], warm_in[:], ACT.Exp)
 
-        def quantise(name, grouped, tag=None):
-            words = grouped.shape[1] // PACK
-            codes = tile([P, words], U32, name + "_codes", tag)
-            scales = tile([P, words], U8, name + "_scales")
-            nc.vector.quantize_mx(out=codes[:].bitcast(FP8X4), scales=scales[:], in_=grouped[:])
+        def quantise(name, grouped, codes):
+            scales = tile([P, grouped.shape[1] // PACK], U8, name + "_scales")
+            nc.vector.quantize_mx(out=codes.bitcast(FP8X4), scales=scales[:], in_=grouped[:])
             return codes, scales
 
         grouped_q = []
@@ -81,8 +79,8 @@ def tile_attend_readtangent_kernel(tc, query, dquery, keys_words, keys_scales, s
         nc.vector.tensor_copy(key_words[:], key_word_pool[:].bitcast(U32).indirect(offsets[:]))
         key_scales = tile([P, I], U8, "key_scales")
         nc.vector.tensor_copy(key_scales[:], key_scale_pool[:].indirect(offsets[:]))
-        quant_q = quantise("q", grouped_q[0])
-        quant_dq = quantise("dq", grouped_q[1])
+        quant_q = quantise("q", grouped_q[0], tile([P, Q], U32, "q_codes")[:])
+        quant_dq = quantise("dq", grouped_q[1], tile([P, Q], U32, "dq_codes")[:])
 
         val_pool = []
         for blk in range(BLOCKS):
@@ -122,7 +120,9 @@ def tile_attend_readtangent_kernel(tc, query, dquery, keys_words, keys_scales, s
             nc.vector.tensor_copy(picked[:], val_pool[blk][:].indirect(offsets[:]))
             turn(picked, grouped)
 
-        grouped_w0 = tile([P, 2 * WIDTH], BF16, "grouped_w0")
+        val_bf16 = tile([P, T], BF16, "val_bf16")
+        nc.scalar.activation(val_bf16[:], val_pool[1][:], ACT.Copy)
+        grouped_w0 = tile([P, 2 * WIDTH], BF16, "grouped_w0", "val1")
         grouped_12 = tile([P, 2 * WIDTH], BF16, "grouped_12")
         grouped_3 = tile([P, WIDTH], BF16, "grouped_3")
 
@@ -132,6 +132,8 @@ def tile_attend_readtangent_kernel(tc, query, dquery, keys_words, keys_scales, s
         p = tile([P, I], F32, "p")
         row_sum = tile([P, 1], F32, "row_sum")
         nc.scalar.activation(p[:], a_bank[:], ACT.Exp, bias=neg_max[:], accum_out=row_sum[:])
+        picked1 = tile([P, I], BF16, "picked1")
+        nc.scalar.activation(picked1[:], val_bf16[:].indirect(offsets[:]), ACT.Copy)
         scratch = tile([P, I + 1], F32, "scratch", "val0")
         pb, inv_sum = scratch[:, :I], scratch[:, I:]
         nc.vector.reciprocal(inv_sum, row_sum[:])
@@ -151,12 +153,13 @@ def tile_attend_readtangent_kernel(tc, query, dquery, keys_words, keys_scales, s
         nc.vector.scalar_tensor_tensor(dw[:], b_bank[:], mean_b[:], w_size[:], ALU.subtract, ALU.mult)
         turn(dw, grouped_w0[:, :WIDTH])
 
-        gather_vals(1, grouped_12[:, :WIDTH])
+        turn(picked1, grouped_12[:, :WIDTH])
         gather_vals(2, grouped_12[:, WIDTH:])
-        quant_w0 = quantise("w0", grouped_w0, "val2")
         gather_vals(3, grouped_3[:])
-        quant_12 = quantise("v12", grouped_12, "val3")
-        quant_3 = quantise("v3", grouped_3)
+        held_codes = tile([P, 4 * P], U32, "held_codes", "val3")
+        quant_w0 = quantise("w0", grouped_w0, held_codes[:, : 2 * P])
+        quant_12 = quantise("v12", grouped_12, held_codes[:, 2 * P :])
+        quant_3 = quantise("v3", grouped_3, tile([P, P], U32, "v3_codes")[:])
 
         result = tile([P, E], F32, "result")
         for first, count, quant, at in ((0, 1, quant_w0, P), (1, 2, quant_12, 0), (3, 1, quant_3, 0)):

from contextlib import ExitStack

import concourse.mybir as mybir
from concourse.masks import make_identity

E, T, I, Q = 512, 2048, 512, 128
FLOPS = 3 * 2 * 512 * 512 * 128

F32 = mybir.dt.float32
BF16 = mybir.dt.bfloat16
I32 = mybir.dt.int32
U32 = mybir.dt.uint32
U16 = mybir.dt.uint16
U8 = mybir.dt.uint8
FP8X4 = mybir.dt.float8_e4m3fn_x4
ALU = mybir.AluOpType
ACT = mybir.ActivationFunctionType
AX = mybir.AxisListType

P = 128
PACK = 4
BLOCKS = E // P
WIDTH = P * PACK


def tile_attend_readtangent_kernel(tc, query, dquery, keys_words, keys_scales, size, vals, offs, out):
    nc = tc.nc
    with ExitStack() as ctx:
        sb = ctx.enter_context(tc.tile_pool(name="sb", bufs=1))
        ps = ctx.enter_context(tc.psum_pool(name="ps", bufs=1))
        ps_turn = ctx.enter_context(tc.psum_pool(name="ps_turn", bufs=2))

        def tile(shape, dtype, name, tag=None):
            return sb.tile(shape, dtype, name=name, tag=tag or name, align_bytes=64)

        offsets = tile([P, I // 16], U16, "offsets")
        nc.sync.dma_start(offsets[:], offs)

        key_scale_pool = tile([P, T], U8, "key_scale_pool")
        nc.vector.memset(key_scale_pool[:].bitcast(I32), 0)
        for quad in range(4):
            nc.sync.dma_start(
                key_scale_pool[32 * quad : 32 * quad + 4, :].bitcast(I32),
                keys_scales[0, 4 * quad : 4 * quad + 4, :].bitcast(I32),
            )

        key_word_pool = tile([P, T], I32, "key_word_pool")
        nc.sync.dma_start(key_word_pool[:], keys_words[0].rearrange("p n t -> p (n t)").bitcast(I32))

        raw_q = []
        for name, src, tag in (("raw_q", query, "val2"), ("raw_dq", dquery, "val3")):
            raw = tile([P, PACK, Q], F32, name, tag)
            nc.sync.dma_start(raw[:], src.rearrange("(p j) q -> p j q", j=PACK))
            raw_q.append(raw)

        size_cols = tile([P, PACK], F32, "size_cols")
        nc.gpsimd.dma_start(size_cols[:], size[0].rearrange("(p t) -> p t", t=PACK))

        ident = tile([P, P], F32, "ident")
        make_identity(nc, ident[:])

        warm_in = tile([P, 1], F32, "warm_in", "val0")
        warm_out = tile([P, 1], F32, "warm_out", "val1")
        nc.vector.memset(warm_in[:], 0.0)
        nc.scalar.activation(warm_out[:], warm_in[:], ACT.Exp)

        def quantise(name, grouped, codes):
            scales = tile([P, grouped.shape[1] // PACK], U8, name + "_scales")
            nc.vector.quantize_mx(out=codes.bitcast(FP8X4), scales=scales[:], in_=grouped[:])
            return codes, scales

        grouped_q = []
        for name, raw in zip(("grouped_q", "grouped_dq"), raw_q):
            grouped = tile([P, WIDTH], BF16, name)
            nc.scalar.copy(grouped[:].rearrange("p (q j) -> p q j", j=PACK), raw[:].rearrange("p j q -> p q j"))
            grouped_q.append(grouped)

        key_words = tile([P, I], U32, "key_words")
        nc.vector.tensor_copy(key_words[:], key_word_pool[:].bitcast(U32).indirect(offsets[:]))
        key_scales = tile([P, I], U8, "key_scales")
        nc.vector.tensor_copy(key_scales[:], key_scale_pool[:].indirect(offsets[:]))
        quant_q = quantise("q", grouped_q[0], tile([P, Q], U32, "q_codes")[:])
        quant_dq = quantise("dq", grouped_q[1], tile([P, Q], U32, "dq_codes")[:])

        val_pool = []
        for blk in range(BLOCKS):
            pool_blk = tile([P, T], F32, "val_pool%d" % blk, "val%d" % blk)
            nc.sync.dma_start(pool_blk[:], vals[blk * P : (blk + 1) * P, :])
            val_pool.append(pool_blk)

        def product(bank, lhs, lhs_cols, rhs, rhs_cols):
            nc.tensor.matmul_mx(
                out=bank,
                lhsT=lhs[0][:, lhs_cols].bitcast(FP8X4), lhsT_scale=lhs[1][:, lhs_cols],
                rhs=rhs[0][:, rhs_cols].bitcast(FP8X4), rhs_scale=rhs[1][:, rhs_cols],
                start=True, stop=True,
            )

        a_bank = ps.tile([P, I], F32, name="a_bank")
        b_bank = ps.tile([P, I], F32, name="b_bank")
        product(a_bank[:], quant_q, slice(0, Q), (key_words, key_scales), slice(0, I))
        product(b_bank[:], quant_dq, slice(0, Q), (key_words, key_scales), slice(0, I))

        size_rows = ps.tile([P, PACK, P], F32, name="size_rows")
        for t in range(PACK):
            nc.tensor.transpose(size_rows[:, t, :], size_cols[:, t : t + 1].to_broadcast([P, P]), ident[:])

        def turn(rows, grouped):
            words = rows[:].bitcast(F32)
            turned = ps_turn.tile([P, 2, P], F32, name="turned")
            for u in range(2):
                nc.tensor.transpose(turned[:, u, :], words[:, u : I // 2 : 2], ident[:])
            nc.scalar.copy(
                grouped.bitcast(F32).rearrange("p (c u) -> p c u", u=2),
                turned[:].rearrange("p u c -> p c u"),
            )

        def gather_vals(blk, grouped):
            picked = tile([P, I], BF16, "picked%d" % blk)
            nc.vector.tensor_copy(picked[:], val_pool[blk][:].indirect(offsets[:]))
            turn(picked, grouped)

        val_bf16 = tile([P, T], BF16, "val_bf16")
        nc.scalar.activation(val_bf16[:], val_pool[1][:], ACT.Copy)
        grouped_w0 = tile([P, 2 * WIDTH], BF16, "grouped_w0", "val1")
        grouped_12 = tile([P, 2 * WIDTH], BF16, "grouped_12")
        grouped_3 = tile([P, WIDTH], BF16, "grouped_3")

        neg_max = tile([P, 1], F32, "neg_max")
        nc.vector.tensor_reduce(neg_max[:], a_bank[:], AX.X, ALU.max, negate=True)
        gather_vals(0, grouped_w0[:, WIDTH:])
        p = tile([P, I], F32, "p")
        row_sum = tile([P, 1], F32, "row_sum")
        nc.scalar.activation(p[:], a_bank[:], ACT.Exp, bias=neg_max[:], accum_out=row_sum[:])
        picked1 = tile([P, I], BF16, "picked1")
        nc.scalar.activation(picked1[:], val_bf16[:].indirect(offsets[:]), ACT.Copy)
        scratch = tile([P, I + 1], F32, "scratch", "val0")
        pb, inv_sum = scratch[:, :I], scratch[:, I:]
        nc.vector.reciprocal(inv_sum, row_sum[:])
        pb_sum = tile([P, 1], F32, "pb_sum")
        nc.vector.scalar_tensor_tensor(pb, p[:], 1.0, b_bank[:], ALU.mult, ALU.mult, accum_out=pb_sum[:])
        w_size = tile([P, I], F32, "w_size")
        nc.vector.scalar_tensor_tensor(
            w_size[:].rearrange("q (s t) -> q s t", t=PACK),
            p[:].rearrange("q (s t) -> q s t", t=PACK),
            inv_sum,
            size_rows[:].rearrange("q t s -> q s t"),
            ALU.mult, ALU.mult,
        )
        mean_b = tile([P, 1], F32, "mean_b")
        nc.vector.tensor_tensor(mean_b[:], pb_sum[:], inv_sum, ALU.mult)
        dw = tile([P, I], BF16, "dw")
        nc.vector.scalar_tensor_tensor(dw[:], b_bank[:], mean_b[:], w_size[:], ALU.subtract, ALU.mult)
        turn(dw, grouped_w0[:, :WIDTH])

        turn(picked1, grouped_12[:, :WIDTH])
        gather_vals(2, grouped_12[:, WIDTH:])
        gather_vals(3, grouped_3[:])
        held_codes = tile([P, 4 * P], U32, "held_codes", "val3")
        quant_w0 = quantise("w0", grouped_w0, held_codes[:, : 2 * P])
        quant_12 = quantise("v12", grouped_12, held_codes[:, 2 * P :])
        quant_3 = quantise("v3", grouped_3, tile([P, P], U32, "v3_codes")[:])

        result = tile([P, E], F32, "result")
        for first, count, quant, at in ((0, 1, quant_w0, P), (1, 2, quant_12, 0), (3, 1, quant_3, 0)):
            bank = ps.tile([P, count * P], F32, name="out%d" % first)
            product(bank[:], quant_w0, slice(0, Q), quant, slice(at, at + count * P))
            cols = slice(first * P, (first + count) * P)
            nc.scalar.copy(result[:, cols], bank[:])
            nc.sync.dma_start(out[:, cols], result[:, cols])
